import numpy as np
import ml_dtypes


def mxq(x, axis, fmt="e4m3"):
    dtype, down = {"e4m3": (ml_dtypes.float8_e4m3fn, 7), "e5m2": (ml_dtypes.float8_e5m2, 14)}[fmt]
    v = np.moveaxis(np.asarray(x, np.float32).astype(ml_dtypes.bfloat16).astype(np.float64), axis, -1)
    blocks = v.reshape(v.shape[:-1] + (-1, 32))
    amax = np.abs(blocks).max(-1, keepdims=True)
    byte = np.maximum(np.where(amax > 0, np.frexp(amax)[1] - 1 + 127, 0) - down, 1)
    scale = np.exp2(byte - 127.0)
    codes = (blocks / scale).astype(np.float32).astype(dtype).astype(np.float64)
    return np.moveaxis((codes * scale).reshape(v.shape), -1, axis)


WIDE = False


def mx_kscale(k):
    if not WIDE:
        return np.ones(k)
    levels = np.array([10, -10, 5, -5, 0])
    if k % 512:
        return np.exp2(np.random.permutation(np.resize(levels, k // 32))).repeat(32)
    a = np.empty((k // 512, 16))
    for p in range(k // 512):
        a[p, :8] = np.random.permutation(np.resize(levels, 8))
        for g in range(8):
            far = levels[np.abs(levels - a[p, g]) >= 10]
            a[p, g + 8] = far[np.random.randint(len(far))]
    return np.exp2(a.ravel()).repeat(32)


def f64(x):
    return np.asarray(x).astype(np.float64)


def striped(idx):
    return np.tile(idx.reshape(-1, 16).T, (8, 1)).astype(np.uint16)


def unstriped(offs):
    return offs[:16].T.reshape(-1).astype(np.int64)


def striped8(idx):
    return np.concatenate([x.reshape(-1, 16).T for x in idx]).astype(np.uint16)


def runs(offs, k):
    lists = np.stack([offs[16 * r : 16 * r + 16].T.reshape(-1) for r in range(8)]).astype(np.int64)
    return lists[np.arange(k) % 512 // 64]


def pack_weight(w):
    k, n = w.shape
    w = f64(np.asarray(w, np.float32).astype(ml_dtypes.bfloat16)).reshape(k // 32, 32, n)
    amax = np.abs(w).max(1)
    byte = np.clip(np.where(amax > 0, np.frexp(amax)[1] - 1 + 127 - 7, 1), 1, 254)
    scaled = (w * np.exp2(127.0 - byte)[:, None, :]).reshape(k, n).astype(np.float32)
    words = np.ascontiguousarray(scaled.reshape(k // 512, 128, 4, n).transpose(0, 1, 3, 2)).astype(ml_dtypes.float8_e4m3fn).view(np.uint8)
    return words, np.ascontiguousarray(byte.astype(np.uint8).reshape(k // 512, 16, n))


def unpack_weight(words, scales):
    g, p, n, _ = words.shape
    vals = np.ascontiguousarray(words).view(ml_dtypes.float8_e4m3fn).astype(np.float64) * np.repeat(np.exp2(scales.astype(np.float64) - 127.0), 8, axis=1)[..., None]
    return vals.transpose(0, 1, 3, 2).reshape(g * 512, n)


def sigmoid(v):
    return 1.0 / (1.0 + np.exp(-np.maximum(v, -700.0)))

def planes(y):
    n, m = y.shape
    v = y.astype(np.float32).astype(ml_dtypes.bfloat16).astype(np.float64).reshape(n // 32, 32, m)
    top = np.abs(v).max(1)
    byte = np.clip(np.where(top > 0, np.frexp(top)[1] - 1 + 127 - 7, 1), 1, 254)
    codes = (v * np.exp2(127.0 - byte)[:, None, :]).reshape(n, m).astype(np.float32).astype(ml_dtypes.float8_e4m3fn).view(np.uint8)
    words = codes.reshape(n // 512, 128, 4, m).transpose(0, 1, 3, 2)
    return np.ascontiguousarray(words), np.ascontiguousarray(byte.astype(np.uint8).reshape(n // 512, 16, m))


K, T, S, H, J, W = 512, 2048, 512, 512, 512, 256


def setup_inputs():
    n = np.random.standard_normal
    s = mx_kscale(K)[:, None]
    u = mx_kscale(S)
    packed_xT = pack_weight(n((K, T)) * s)
    packed_w1 = pack_weight(n((K, H)) / np.sqrt(K) / s)
    perm = np.stack([np.random.permutation(S) for _ in range(8)])
    return {
        "x_words": packed_xT[0],
        "x_scales": packed_xT[1],
        "w1_words": packed_w1[0],
        "w1_scales": packed_w1[1],
        "tab": np.random.uniform(0.4, 1.4, (H, J)).astype(np.float32),
        "ga": (np.random.uniform(0.5, 1.5, (H, 1)) * u[:, None]).astype(np.float32),
        "gb": (np.random.uniform(0.5, 1.5, (H, 1)) / u[:, None]).astype(np.float32),
        "offs": striped(np.random.permutation(T)[:S]),
        "n1": striped8(np.stack([np.random.permutation(S) for _ in range(8)])),
        "n2": striped8(np.stack([np.random.permutation(S) for _ in range(8)])),
        "n3": striped8(np.random.randint(0, J, (8, S))),
        "n4": striped8(np.stack([np.random.permutation(S) for _ in range(8)])),
        "n5": striped8(perm[:, :W]),
        "n6": striped8(perm[:, W:]),
    }


def reference(x_words, x_scales, w1_words, w1_scales, tab, ga, gb, offs, n1, n2, n3, n4, n5, n6):
    xq = unpack_weight(x_words, x_scales)[:, unstriped(offs)]
    y = unpack_weight(w1_words, w1_scales).T @ xq
    z = f64(ga) * (y * (sigmoid(y[np.arange(H)[:, None], runs(n1, H)] - (y[np.arange(H)[:, None], runs(n2, H)]))))
    z2 = f64(gb) * (y * (f64(tab)[np.arange(H)[:, None], runs(n3, H)]) - (0.5 * (y[np.arange(H)[:, None], runs(n4, H)])))
    s = 0.0625 * ((mxq(z, 0, "e4m3").T @ mxq(z2, 0, "e4m3")))
    pa = s[np.arange(S)[:, None], runs(n5, S)]
    pb = s[np.arange(S)[:, None], runs(n6, S)]
    rb = np.maximum(0.5 * pa, pb)
    ra = pb - pa
    ds = np.zeros((S, S))
    ds[np.arange(S)[:, None], runs(n5, S)] = ra
    out = ds.copy()
    out[np.arange(S)[:, None], runs(n6, S)] = rb
    return (out,) + planes(out)

@@ -1,0 +1,254 @@
+from contextlib import ExitStack
+
+import concourse.mybir as mybir
+
+F32 = mybir.dt.float32
+BF16 = mybir.dt.bfloat16
+I32 = mybir.dt.int32
+U32 = mybir.dt.uint32
+U16 = mybir.dt.uint16
+U8 = mybir.dt.uint8
+FP8X4 = mybir.dt.float8_e4m3fn_x4
+ALU = mybir.AluOpType
+ACT = mybir.ActivationFunctionType
+
+P = 128
+PACK = 4
+T = 2048
+S = 512
+HALF = S // 2
+FLOPS = 2 * 2 * 512 * 512 * 512
+
+
+def tile_picked_selfcmpkindglift_none_po_kernel(
+    tc, x_words, x_scales, w1_words, w1_scales, tab, ga, gb, offs, n1, n2, n3, n4, n5, n6, out_0, out_1, out_2
+):
+    nc = tc.nc
+    with ExitStack() as ctx:
+        lists = ctx.enter_context(tc.tile_pool(name="lists", bufs=1))
+        sb = ctx.enter_context(tc.tile_pool(name="sb", bufs=1))
+        psum = ctx.enter_context(tc.psum_pool(name="psum", bufs=1))
+
+        def load_list(source, name):
+            tile = lists.tile([P, source.shape[1]], U16, name=name)
+            nc.sync.dma_start(tile[:], source)
+            return tile
+
+        def load_scale_rows(tile, source):
+            for q in range(4):
+                nc.sync.dma_start(
+                    tile[32 * q : 32 * q + 4, :].bitcast(I32), source[0, 4 * q : 4 * q + 4, :].bitcast(I32)
+                )
+
+        def half(list_tile, c):
+            return list_tile[:, c * (HALF // 16) : (c + 1) * (HALF // 16)]
+
+        def cols(c):
+            return slice(c * HALF, (c + 1) * HALF)
+
+        warm = sb.tile([P, 2], F32)
+        nc.gpsimd.memset(warm[:, 0:1], 0.0)
+        nc.scalar.activation(warm[:, 1:2], warm[:, 0:1], ACT.Sigmoid)
+
+        offs_l = load_list(offs, "offs_l")
+        xs = sb.tile([P, T], U8)
+        nc.vector.memset(xs[:].bitcast(I32), 0)
+        load_scale_rows(xs, x_scales)
+        xw = sb.tile([P, T], U32)
+        nc.sync.dma_start(xw[:].bitcast(I32), x_words[0].rearrange("p c r -> p (c r)").bitcast(I32))
+        ww = sb.tile([P, S], I32)
+        nc.sync.dma_start(ww[:], w1_words[0].rearrange("p c r -> p (c r)").bitcast(I32))
+        ws = sb.tile([P, S], U8)
+        nc.vector.memset(ws[:].bitcast(I32), 0)
+        load_scale_rows(ws, w1_scales)
+        n2_l = load_list(n2, "n2_l")
+        n1_l = load_list(n1, "n1_l")
+        gb4 = sb.tile([P, PACK], F32)
+        nc.sync.dma_start(gb4[:], gb.rearrange("(p t) o -> p (t o)", t=PACK))
+        ga4 = sb.tile([P, PACK], F32)
+        nc.sync.dma_start(ga4[:], ga.rearrange("(p t) o -> p (t o)", t=PACK))
+        tab_rows = tab.rearrange("(p t) j -> p t j", t=PACK)
+        tabs = []
+        for t in range(PACK):
+            tab_t = sb.tile([P, S], F32, name=f"tab{t}")
+            nc.sync.dma_start(tab_t[:], tab_rows[:, t, :])
+            tabs.append(tab_t)
+        n3_l = load_list(n3, "n3_l")
+        n4_l = load_list(n4, "n4_l")
+        n5_l = load_list(n5, "n5_l")
+        n6_l = load_list(n6, "n6_l")
+
+        xs_g = sb.tile([P, S], U8, align_bytes=64)
+        nc.vector.tensor_copy(xs_g[:], xs[:].indirect(offs_l[:]))
+        ww_d = sb.tile([P, S], I32, align_bytes=64)
+        nc.vector.tensor_copy(
+            ww_d[:].rearrange("p (t m) -> p m t", t=PACK), ww[:].rearrange("p (m t) -> p m t", t=PACK)
+        )
+        xw_g = sb.tile([P, S], U32, align_bytes=64)
+        nc.vector.tensor_copy(xw_g[:], xw[:].indirect(offs_l[:]))
+        ws_d = sb.tile([P, S], U8, align_bytes=64)
+        nc.vector.tensor_copy(
+            ws_d[:].rearrange("p (t m) -> p t m", t=PACK), ws[:].rearrange("p (m t) -> p t m", t=PACK)
+        )
+
+        gb_half = sb.tile([P, PACK], F32)
+        nc.scalar.mul(gb_half[:], gb4[:], -0.5)
+
+        y_ps, y_sb = [], []
+        for t in range(PACK):
+            bank = psum.tile([P, S], F32, name=f"y_ps{t}")
+            m = slice(t * P, (t + 1) * P)
+            nc.tensor.matmul_mx(
+                out=bank[:], lhsT=ww_d[:, m].bitcast(FP8X4), lhsT_scale=ws_d[:, m],
+                rhs=xw_g[:].bitcast(FP8X4), rhs_scale=xs_g[:], start=True, stop=True,
+            )
+            y_t = sb.tile([P, S], F32, name=f"y{t}")
+            nc.scalar.copy(y_t[:], bank[:])
+            y_ps.append(bank)
+            y_sb.append(y_t)
+
+        diff = sb.tile([P, PACK, S], F32)
+        for t in range(PACK):
+            at_n2 = sb.tile([P, S], F32, name=f"at_n2_{t}")
+            for c in range(2):
+                nc.vector.tensor_copy(at_n2[:, cols(c)], y_sb[t][:].indirect(half(n2_l, c)))
+            for c in range(2):
+                nc.vector.tensor_tensor(
+                    diff[:, t, cols(c)], y_sb[t][:].indirect(half(n1_l, c)), at_n2[:, cols(c)], ALU.subtract
+                )
+
+        y_gb, y_half = [], []
+        for t in range(PACK):
+            y_gb_t = sb.tile([P, S], F32, name=f"y_gb{t}")
+            nc.scalar.activation(y_gb_t[:], y_ps[t][:], ACT.Copy, scale=gb4[:, t : t + 1])
+            y_half_t = sb.tile([P, S], F32, name=f"y_half{t}")
+            nc.scalar.activation(y_half_t[:], y_ps[t][:], ACT.Copy, scale=gb_half[:, t : t + 1])
+            y_gb.append(y_gb_t)
+            y_half.append(y_half_t)
+
+        y_ga = sb.tile([P, PACK, S], F32)
+        for t in range(PACK):
+            nc.scalar.activation(y_ga[:, t, :], y_ps[t][:], ACT.Copy, scale=ga4[:, t : t + 1])
+        y_ga_w = sb.tile([P, PACK, P, PACK], F32)
+        nc.scalar.copy(
+            y_ga_w[:].rearrange("p u m t -> p m t u"), y_ga[:].rearrange("p t (m u) -> p m t u", u=PACK)
+        )
+        gate_w = sb.tile([P, PACK, P, PACK], F32)
+        nc.scalar.activation(
+            gate_w[:].rearrange("p u m t -> p m t u"), diff[:].rearrange("p t (m u) -> p m t u", u=PACK), ACT.Sigmoid
+        )
+
+        prods = [sb.tile([P, HALF], F32, name=f"prod{i}") for i in range(3)]
+        z2_bf = []
+        for c in range(2):
+            z2_c = sb.tile([P, PACK, HALF], F32, name=f"z2_{c}")
+            for t in range(PACK):
+                prod = prods[(c * PACK + t) % 3]
+                nc.vector.tensor_tensor(prod[:], tabs[t][:].indirect(half(n3_l, c)), y_gb[t][:, cols(c)], ALU.mult)
+                nc.vector.tensor_tensor(z2_c[:, t, :], y_half[t][:].indirect(half(n4_l, c)), prod[:], ALU.add)
+            z2_bf_c = sb.tile([P, HALF * PACK], BF16, name=f"z2_bf{c}", align_bytes=64)
+            nc.scalar.copy(
+                z2_bf_c[:].rearrange("p (c i t) -> p c t i", i=4, t=PACK),
+                z2_c[:].rearrange("p t (c i) -> p c t i", i=4),
+            )
+            z2_bf.append(z2_bf_c)
+
+        z_w = sb.tile([P, S], U32, align_bytes=64)
+        z_s = sb.tile([P, S], U8, align_bytes=64)
+        z2_w = sb.tile([P, S], U32, align_bytes=64)
+        z2_s = sb.tile([P, S], U8, align_bytes=64)
+        z_bf = sb.tile([P, 2 * S], BF16, align_bytes=64)
+
+        def make_z(u, stage):
+            nc.vector.tensor_tensor(
+                stage,
+                gate_w[:, u].rearrange("p m t -> p (m t)"),
+                y_ga_w[:, u].rearrange("p m t -> p (m t)"),
+                ALU.mult,
+            )
+
+        def quant_z(u, stage):
+            m = slice(u * P, (u + 1) * P)
+            nc.vector.quantize_mx(out=z_w[:, m].bitcast(FP8X4), scales=z_s[:, m], in_=stage)
+
+        def quant_z2(c):
+            nc.vector.quantize_mx(out=z2_w[:, cols(c)].bitcast(FP8X4), scales=z2_s[:, cols(c)], in_=z2_bf[c][:])
+
+        stages = [z_bf[:, 0:S], z_bf[:, S : 2 * S], z2_bf[1][:, 0:S], z2_bf[1][:, S : 2 * S]]
+        make_z(0, stages[0])
+        quant_z2(0)
+        quant_z(0, stages[0])
+        make_z(1, stages[1])
+        quant_z2(1)
+        quant_z(1, stages[1])
+        make_z(2, stages[2])
+        make_z(3, stages[3])
+        quant_z(2, stages[2])
+        quant_z(3, stages[3])
+
+        s_sb = []
+        for u in range(PACK):
+            bank = psum.tile([P, S], F32, name=f"s_ps{u}")
+            m = slice(u * P, (u + 1) * P)
+            nc.tensor.matmul_mx(
+                out=bank[:], lhsT=z_w[:, m].bitcast(FP8X4), lhsT_scale=z_s[:, m],
+                rhs=z2_w[:].bitcast(FP8X4), rhs_scale=z2_s[:], start=True, stop=True,
+            )
+            s_u = sb.tile([P, S], F32, name=f"s{u}")
+            nc.scalar.activation(s_u[:], bank[:], ACT.Copy, scale=0.0625)
+            s_sb.append(s_u)
+
+        out_rows = out_0.rearrange("(p t) j -> p t j", t=PACK)
+        out_bf = sb.tile([P, S, PACK], BF16, align_bytes=64)
+        neg, gap, pos, over, res = [], [], [], [], []
+        for u in range(PACK):
+            neg.append(sb.tile([P, HALF], F32, name=f"neg{u}"))
+            gap.append(sb.tile([P, HALF], F32, name=f"gap{u}"))
+            pos.append(sb.tile([P, HALF], F32, name=f"pos{u}"))
+            over.append(sb.tile([P, HALF], F32, name=f"over{u}"))
+            res.append(sb.tile([P, S], F32, name=f"res{u}"))
+
+        def fetch_a(u):
+            nc.vector.tensor_scalar(neg[u][:], s_sb[u][:].indirect(n5_l[:]), -0.5, 0.0, ALU.mult, ALU.add)
+            nc.scalar.activation(pos[u][:], neg[u][:], ACT.Copy, scale=-1.0)
+
+        def fetch_b(u):
+            nc.vector.tensor_tensor(gap[u][:], s_sb[u][:].indirect(n6_l[:]), neg[u][:], ALU.add)
+            nc.scalar.activation(over[u][:], gap[u][:], ACT.Relu)
+
+        def put_a(u):
+            nc.vector.tensor_tensor(res[u][:].indirect(n5_l[:]), gap[u][:], neg[u][:], ALU.add)
+
+        def put_b(u):
+            nc.vector.tensor_tensor(res[u][:].indirect(n6_l[:]), over[u][:], pos[u][:], ALU.add)
+            nc.sync.dma_start(out_rows[:, u, :], res[u][:])
+
+        def round_rows(u, c):
+            nc.scalar.copy(out_bf[:, c, u], res[u][:, c])
+
+        fetch_a(0)
+        fetch_b(0)
+        for u in range(PACK - 1):
+            fetch_a(u + 1)
+            put_a(u)
+            fetch_b(u + 1)
+            if u == PACK - 2:
+                put_a(u + 1)
+            put_b(u)
+            round_rows(u, slice(0, S))
+        put_b(PACK - 1)
+
+        out_w = sb.tile([P, S], U32, align_bytes=64)
+        out_s = sb.tile([P, S], U8, align_bytes=64)
+        words_out = out_1[0].rearrange("p c r -> p (c r)").bitcast(I32)
+        for c in range(2):
+            round_rows(PACK - 1, cols(c))
+            nc.vector.quantize_mx(
+                out=out_w[:, cols(c)].bitcast(FP8X4), scales=out_s[:, cols(c)],
+                in_=out_bf[:, cols(c), :].rearrange("p c t -> p (c t)"),
+            )
+            nc.sync.dma_start(words_out[:, cols(c)], out_w[:, cols(c)].bitcast(I32))
+        for q in range(4):
+            nc.sync.dma_start(
+                out_2[0, 4 * q : 4 * q + 4, :].bitcast(I32), out_s[32 * q : 32 * q + 4, :].bitcast(I32)
+            )

@@ -17,6 +17,7 @@ PACK = 4
 T = 2048
 S = 512
 HALF = S // 2
+ORDER = (0, 2, 3, 1)
 FLOPS = 2 * 2 * 512 * 512 * 512
 
 
@@ -34,9 +35,9 @@ def tile_picked_selfcmpkindglift_none_po_kernel(
             nc.sync.dma_start(tile[:], source)
             return tile
 
-        def load_scale_rows(tile, source):
-            for q in range(4):
-                nc.sync.dma_start(
+        def load_scale_rows(queues, tile, source):
+            for q, queue in enumerate(queues):
+                queue.dma_start(
                     tile[32 * q : 32 * q + 4, :].bitcast(I32), source[0, 4 * q : 4 * q + 4, :].bitcast(I32)
                 )
 
@@ -46,21 +47,20 @@ def tile_picked_selfcmpkindglift_none_po_kernel(
         def cols(c):
             return slice(c * HALF, (c + 1) * HALF)
 
-        warm = sb.tile([P, 2], F32)
-        nc.gpsimd.memset(warm[:, 0:1], 0.0)
-        nc.scalar.activation(warm[:, 1:2], warm[:, 0:1], ACT.Sigmoid)
-
-        offs_l = load_list(offs, "offs_l")
         xs = sb.tile([P, T], U8)
         nc.vector.memset(xs[:].bitcast(I32), 0)
-        load_scale_rows(xs, x_scales)
-        xw = sb.tile([P, T], U32)
-        nc.sync.dma_start(xw[:].bitcast(I32), x_words[0].rearrange("p c r -> p (c r)").bitcast(I32))
-        ww = sb.tile([P, S], I32)
-        nc.sync.dma_start(ww[:], w1_words[0].rearrange("p c r -> p (c r)").bitcast(I32))
         ws = sb.tile([P, S], U8)
         nc.vector.memset(ws[:].bitcast(I32), 0)
-        load_scale_rows(ws, w1_scales)
+        offs_l = load_list(offs, "offs_l")
+        xw = sb.tile([P, T], U32, tag="x_word_bytes", align_bytes=64)
+        nc.sync.dma_start(xw[:].bitcast(I32), x_words[0].rearrange("p c r -> p (c r)").bitcast(I32))
+        load_scale_rows([nc.sync] * 4, xs, x_scales)
+        ww = sb.tile([P, S], I32)
+        nc.sync.dma_start(ww[:], w1_words[0].rearrange("p c r -> p (c r)").bitcast(I32))
+        load_scale_rows([nc.sync, nc.sync, nc.gpsimd, nc.gpsimd], ws, w1_scales)
+        warm = sb.tile([P, 2], F32)
+        nc.vector.memset(warm[:, 0:1], 0.0)
+        nc.scalar.activation(warm[:, 1:2], warm[:, 0:1], ACT.Sigmoid)
         n2_l = load_list(n2, "n2_l")
         n1_l = load_list(n1, "n1_l")
         gb4 = sb.tile([P, PACK], F32)
@@ -78,33 +78,39 @@ def tile_picked_selfcmpkindglift_none_po_kernel(
         n5_l = load_list(n5, "n5_l")
         n6_l = load_list(n6, "n6_l")
 
-        xs_g = sb.tile([P, S], U8, align_bytes=64)
-        nc.vector.tensor_copy(xs_g[:], xs[:].indirect(offs_l[:]))
-        ww_d = sb.tile([P, S], I32, align_bytes=64)
-        nc.vector.tensor_copy(
-            ww_d[:].rearrange("p (t m) -> p m t", t=PACK), ww[:].rearrange("p (m t) -> p m t", t=PACK)
-        )
         xw_g = sb.tile([P, S], U32, align_bytes=64)
         nc.vector.tensor_copy(xw_g[:], xw[:].indirect(offs_l[:]))
+        ww_d = sb.tile([P, S], I32, tag="x_word_bytes", align_bytes=64)
         ws_d = sb.tile([P, S], U8, align_bytes=64)
-        nc.vector.tensor_copy(
-            ws_d[:].rearrange("p (t m) -> p t m", t=PACK), ws[:].rearrange("p (m t) -> p t m", t=PACK)
-        )
+
+        def deal(first, last):
+            for dealt, plain in ((ww_d, ww), (ws_d, ws)):
+                nc.vector.tensor_copy(
+                    dealt[:].rearrange("p (t m) -> p m t", t=PACK)[:, :, first:last],
+                    plain[:].rearrange("p (m t) -> p m t", t=PACK)[:, :, first:last],
+                )
+
+        xs_g = sb.tile([P, S], U8, align_bytes=64)
+        nc.vector.tensor_copy(xs_g[:, cols(0)], xs[:].indirect(half(offs_l, 0)))
+        deal(0, 1)
+        nc.vector.tensor_copy(xs_g[:, cols(1)], xs[:].indirect(half(offs_l, 1)))
+        deal(1, PACK)
 
         gb_half = sb.tile([P, PACK], F32)
         nc.scalar.mul(gb_half[:], gb4[:], -0.5)
 
-        y_ps, y_sb = [], []
+        y_ps, y_sb = {}, []
         for t in range(PACK):
-            bank = psum.tile([P, S], F32, name=f"y_ps{t}")
             m = slice(t * P, (t + 1) * P)
-            nc.tensor.matmul_mx(
-                out=bank[:], lhsT=ww_d[:, m].bitcast(FP8X4), lhsT_scale=ws_d[:, m],
-                rhs=xw_g[:].bitcast(FP8X4), rhs_scale=xs_g[:], start=True, stop=True,
-            )
             y_t = sb.tile([P, S], F32, name=f"y{t}")
-            nc.scalar.copy(y_t[:], bank[:])
-            y_ps.append(bank)
+            for c in range(2):
+                bank = psum.tile([P, HALF], F32, name=f"y_ps{t}{c}", tag=f"bank{t}{c}")
+                nc.tensor.matmul_mx(
+                    out=bank[:], lhsT=ww_d[:, m].bitcast(FP8X4), lhsT_scale=ws_d[:, m],
+                    rhs=xw_g[:, cols(c)].bitcast(FP8X4), rhs_scale=xs_g[:, cols(c)], start=True, stop=True,
+                )
+                nc.scalar.copy(y_t[:, cols(c)], bank[:])
+                y_ps[t, c] = bank
             y_sb.append(y_t)
 
         diff = sb.tile([P, PACK, S], F32)
@@ -117,18 +123,22 @@ def tile_picked_selfcmpkindglift_none_po_kernel(
                     diff[:, t, cols(c)], y_sb[t][:].indirect(half(n1_l, c)), at_n2[:, cols(c)], ALU.subtract
                 )
 
+        def scaled(out, t, factor):
+            for c in range(2):
+                nc.scalar.activation(out[:, cols(c)], y_ps[t, c][:], ACT.Copy, scale=factor[:, t : t + 1])
+
         y_gb, y_half = [], []
         for t in range(PACK):
             y_gb_t = sb.tile([P, S], F32, name=f"y_gb{t}")
-            nc.scalar.activation(y_gb_t[:], y_ps[t][:], ACT.Copy, scale=gb4[:, t : t + 1])
+            scaled(y_gb_t, t, gb4)
             y_half_t = sb.tile([P, S], F32, name=f"y_half{t}")
-            nc.scalar.activation(y_half_t[:], y_ps[t][:], ACT.Copy, scale=gb_half[:, t : t + 1])
+            scaled(y_half_t, t, gb_half)
             y_gb.append(y_gb_t)
             y_half.append(y_half_t)
 
         y_ga = sb.tile([P, PACK, S], F32)
         for t in range(PACK):
-            nc.scalar.activation(y_ga[:, t, :], y_ps[t][:], ACT.Copy, scale=ga4[:, t : t + 1])
+            scaled(y_ga[:, t, :], t, ga4)
         y_ga_w = sb.tile([P, PACK, P, PACK], F32)
         nc.scalar.copy(
             y_ga_w[:].rearrange("p u m t -> p m t u"), y_ga[:].rearrange("p t (m u) -> p m t u", u=PACK)
@@ -175,20 +185,20 @@ def tile_picked_selfcmpkindglift_none_po_kernel(
             nc.vector.quantize_mx(out=z2_w[:, cols(c)].bitcast(FP8X4), scales=z2_s[:, cols(c)], in_=z2_bf[c][:])
 
         stages = [z_bf[:, 0:S], z_bf[:, S : 2 * S], z2_bf[1][:, 0:S], z2_bf[1][:, S : 2 * S]]
-        make_z(0, stages[0])
+        make_z(ORDER[0], stages[0])
         quant_z2(0)
-        quant_z(0, stages[0])
-        make_z(1, stages[1])
+        quant_z(ORDER[0], stages[0])
+        make_z(ORDER[1], stages[1])
         quant_z2(1)
-        quant_z(1, stages[1])
-        make_z(2, stages[2])
-        make_z(3, stages[3])
-        quant_z(2, stages[2])
-        quant_z(3, stages[3])
+        quant_z(ORDER[1], stages[1])
+        make_z(ORDER[2], stages[2])
+        make_z(ORDER[3], stages[3])
+        quant_z(ORDER[2], stages[2])
+        quant_z(ORDER[3], stages[3])
 
-        s_sb = []
-        for u in range(PACK):
-            bank = psum.tile([P, S], F32, name=f"s_ps{u}")
+        s_sb = {}
+        for u in ORDER:
+            bank = psum.tile([P, S], F32, name=f"s_ps{u}", tag=f"bank{u}0")
             m = slice(u * P, (u + 1) * P)
             nc.tensor.matmul_mx(
                 out=bank[:], lhsT=z_w[:, m].bitcast(FP8X4), lhsT_scale=z_s[:, m],
@@ -196,7 +206,7 @@ def tile_picked_selfcmpkindglift_none_po_kernel(
             )
             s_u = sb.tile([P, S], F32, name=f"s{u}")
             nc.scalar.activation(s_u[:], bank[:], ACT.Copy, scale=0.0625)
-            s_sb.append(s_u)
+            s_sb[u] = s_u
 
         out_rows = out_0.rearrange("(p t) j -> p t j", t=PACK)
         out_bf = sb.tile([P, S, PACK], BF16, align_bytes=64)
@@ -223,32 +233,31 @@ def tile_picked_selfcmpkindglift_none_po_kernel(
             nc.vector.tensor_tensor(res[u][:].indirect(n6_l[:]), over[u][:], pos[u][:], ALU.add)
             nc.sync.dma_start(out_rows[:, u, :], res[u][:])
 
-        def round_rows(u, c):
-            nc.scalar.copy(out_bf[:, c, u], res[u][:, c])
-
-        fetch_a(0)
-        fetch_b(0)
-        for u in range(PACK - 1):
-            fetch_a(u + 1)
+        last = ORDER[-1]
+        fetch_a(ORDER[0])
+        fetch_b(ORDER[0])
+        for u, following in zip(ORDER, ORDER[1:]):
+            fetch_a(following)
             put_a(u)
-            fetch_b(u + 1)
-            if u == PACK - 2:
-                put_a(u + 1)
+            fetch_b(following)
+            if following == last:
+                put_a(last)
             put_b(u)
-            round_rows(u, slice(0, S))
-        put_b(PACK - 1)
+            nc.scalar.copy(out_bf[:, :, u], res[u][:])
+        put_b(last)
+        nc.vector.tensor_copy(out_bf[:, cols(0), last], res[last][:, cols(0)])
+        nc.scalar.copy(out_bf[:, cols(1), last], res[last][:, cols(1)])
 
         out_w = sb.tile([P, S], U32, align_bytes=64)
         out_s = sb.tile([P, S], U8, align_bytes=64)
         words_out = out_1[0].rearrange("p c r -> p (c r)").bitcast(I32)
         for c in range(2):
-            round_rows(PACK - 1, cols(c))
             nc.vector.quantize_mx(
                 out=out_w[:, cols(c)].bitcast(FP8X4), scales=out_s[:, cols(c)],
                 in_=out_bf[:, cols(c), :].rearrange("p c t -> p (c t)"),
             )
             nc.sync.dma_start(words_out[:, cols(c)], out_w[:, cols(c)].bitcast(I32))
         for q in range(4):
-            nc.sync.dma_start(
+            nc.scalar.dma_start(
                 out_2[0, 4 * q : 4 * q + 4, :].bitcast(I32), out_s[32 * q : 32 * q + 4, :].bitcast(I32)
             )

@@ -14,11 +14,14 @@ ACT = mybir.ActivationFunctionType
 
 P = 128
 PACK = 4
-T = 2048
+QUADRANTS = 4
+TOKENS = 2048
 S = 512
 HALF = S // 2
-ORDER = (0, 2, 3, 1)
-FLOPS = 2 * 2 * 512 * 512 * 512
+LIST_ROWS = 16
+PRODUCT_TILES = 3
+TILE_ORDER = (0, 2, 3, 1)
+FLOPS = 2 * (2 * S * S * S)
 
 
 def tile_picked_selfcmpkindglift_none_po_kernel(
@@ -35,229 +38,261 @@ def tile_picked_selfcmpkindglift_none_po_kernel(
             nc.sync.dma_start(tile[:], source)
             return tile
 
-        def load_scale_rows(queues, tile, source):
-            for q, queue in enumerate(queues):
-                queue.dma_start(
-                    tile[32 * q : 32 * q + 4, :].bitcast(I32), source[0, 4 * q : 4 * q + 4, :].bitcast(I32)
-                )
+        def live_rows(q):
+            return slice(32 * q, 32 * q + 4)
 
-        def half(list_tile, c):
-            return list_tile[:, c * (HALF // 16) : (c + 1) * (HALF // 16)]
+        def scale_rows(scales, q):
+            return scales[0, 4 * q : 4 * q + 4, :].bitcast(I32)
 
-        def cols(c):
-            return slice(c * HALF, (c + 1) * HALF)
+        def load_scales(tile, scales):
+            for q in range(QUADRANTS):
+                nc.sync.dma_start(tile[live_rows(q), :].bitcast(I32), scale_rows(scales, q))
 
-        xs = sb.tile([P, T], U8)
-        nc.vector.memset(xs[:].bitcast(I32), 0)
-        ws = sb.tile([P, S], U8)
-        nc.vector.memset(ws[:].bitcast(I32), 0)
-        offs_l = load_list(offs, "offs_l")
-        xw = sb.tile([P, T], U32, tag="x_word_bytes", align_bytes=64)
-        nc.sync.dma_start(xw[:].bitcast(I32), x_words[0].rearrange("p c r -> p (c r)").bitcast(I32))
-        load_scale_rows([nc.sync] * 4, xs, x_scales)
-        ww = sb.tile([P, S], I32)
-        nc.sync.dma_start(ww[:], w1_words[0].rearrange("p c r -> p (c r)").bitcast(I32))
-        load_scale_rows([nc.sync, nc.sync, nc.gpsimd, nc.gpsimd], ws, w1_scales)
-        warm = sb.tile([P, 2], F32)
-        nc.vector.memset(warm[:, 0:1], 0.0)
-        nc.scalar.activation(warm[:, 1:2], warm[:, 0:1], ACT.Sigmoid)
-        n2_l = load_list(n2, "n2_l")
-        n1_l = load_list(n1, "n1_l")
-        gb4 = sb.tile([P, PACK], F32)
-        nc.sync.dma_start(gb4[:], gb.rearrange("(p t) o -> p (t o)", t=PACK))
-        ga4 = sb.tile([P, PACK], F32)
-        nc.sync.dma_start(ga4[:], ga.rearrange("(p t) o -> p (t o)", t=PACK))
+        def as_words(packed):
+            return packed[0].rearrange("p c r -> p (c r)").bitcast(I32)
+
+        def cols(h):
+            return slice(h * HALF, (h + 1) * HALF)
+
+        def half_list(tile, h):
+            return tile[:, h * (HALF // LIST_ROWS) : (h + 1) * (HALF // LIST_ROWS)]
+
+        def tile_cols(t):
+            return slice(t * P, (t + 1) * P)
+
+        x_scale_window = sb.tile([P, TOKENS], U8)
+        nc.vector.memset(x_scale_window[:].bitcast(I32), 0)
+        w_scale = sb.tile([P, S], U8)
+        nc.vector.memset(w_scale[:].bitcast(I32), 0)
+        x_scale_landing = sb.tile([P, TOKENS], U8)
+        load_scales(x_scale_landing, x_scales)
+        offs_list = load_list(offs, "offs_list")
+        x_word_window = sb.tile([P, TOKENS], U32, tag="x_words_then_kinds")
+        nc.sync.dma_start(x_word_window[:].bitcast(I32), as_words(x_words))
+        load_scales(w_scale, w1_scales)
+        w_word = sb.tile([P, S], I32)
+        nc.sync.dma_start(w_word[:], as_words(w1_words))
         tab_rows = tab.rearrange("(p t) j -> p t j", t=PACK)
-        tabs = []
-        for t in range(PACK):
-            tab_t = sb.tile([P, S], F32, name=f"tab{t}")
-            nc.sync.dma_start(tab_t[:], tab_rows[:, t, :])
-            tabs.append(tab_t)
-        n3_l = load_list(n3, "n3_l")
-        n4_l = load_list(n4, "n4_l")
-        n5_l = load_list(n5, "n5_l")
-        n6_l = load_list(n6, "n6_l")
+        tab_tiles = [sb.tile([P, S], F32, name=f"tab{t}") for t in range(PACK)]
+        n3_list = load_list(n3, "n3_list")
+        nc.sync.dma_start(tab_tiles[0][:], tab_rows[:, 0, :])
+        n2_list = load_list(n2, "n2_list")
+        n1_list = load_list(n1, "n1_list")
+        gb_rows = sb.tile([P, PACK], F32)
+        nc.sync.dma_start(gb_rows[:], gb.rearrange("(p t) o -> p (t o)", t=PACK))
+        ga_rows = sb.tile([P, PACK], F32)
+        nc.sync.dma_start(ga_rows[:], ga.rearrange("(p t) o -> p (t o)", t=PACK))
+        for t in range(1, PACK):
+            nc.sync.dma_start(tab_tiles[t][:], tab_rows[:, t, :])
+        n4_list = load_list(n4, "n4_list")
+        n5_list = load_list(n5, "n5_list")
+        n6_list = load_list(n6, "n6_list")
 
-        xw_g = sb.tile([P, S], U32, align_bytes=64)
-        nc.vector.tensor_copy(xw_g[:], xw[:].indirect(offs_l[:]))
-        ww_d = sb.tile([P, S], I32, tag="x_word_bytes", align_bytes=64)
-        ws_d = sb.tile([P, S], U8, align_bytes=64)
+        for q in range(QUADRANTS):
+            nc.vector.tensor_copy(
+                x_scale_window[live_rows(q), :].bitcast(I32), x_scale_landing[live_rows(q), :].bitcast(I32)
+            )
+        picked_scale = sb.tile([P, S], U8, align_bytes=64)
+        nc.vector.tensor_copy(picked_scale[:], x_scale_window[:].indirect(offs_list[:]))
+        picked_word = sb.tile([P, S], U32, align_bytes=64)
+        nc.vector.tensor_copy(picked_word[:], x_word_window[:].indirect(offs_list[:]))
 
-        def deal(first, last):
-            for dealt, plain in ((ww_d, ww), (ws_d, ws)):
+        w_word_dealt = sb.tile([P, S], I32, align_bytes=64)
+        w_scale_dealt = sb.tile([P, S], U8, align_bytes=64)
+        for tiles in (slice(0, 1), slice(1, PACK)):
+            for dealt, plain in ((w_scale_dealt, w_scale), (w_word_dealt, w_word)):
                 nc.vector.tensor_copy(
-                    dealt[:].rearrange("p (t m) -> p m t", t=PACK)[:, :, first:last],
-                    plain[:].rearrange("p (m t) -> p m t", t=PACK)[:, :, first:last],
+                    dealt[:].rearrange("p (t m) -> p m t", t=PACK)[:, :, tiles],
+                    plain[:].rearrange("p (m t) -> p m t", t=PACK)[:, :, tiles],
                 )
 
-        xs_g = sb.tile([P, S], U8, align_bytes=64)
-        nc.vector.tensor_copy(xs_g[:, cols(0)], xs[:].indirect(half(offs_l, 0)))
-        deal(0, 1)
-        nc.vector.tensor_copy(xs_g[:, cols(1)], xs[:].indirect(half(offs_l, 1)))
-        deal(1, PACK)
+        kinds_0 = sb.tile([P, S], F32, tag="x_words_then_kinds")
+        for h in range(2):
+            nc.vector.tensor_copy(kinds_0[:, cols(h)], tab_tiles[0][:].indirect(half_list(n3_list, h)))
 
-        gb_half = sb.tile([P, PACK], F32)
-        nc.scalar.mul(gb_half[:], gb4[:], -0.5)
+        gb_minus_half = sb.tile([P, PACK], F32)
+        nc.scalar.mul(gb_minus_half[:], gb_rows[:], -0.5)
 
-        y_ps, y_sb = {}, []
+        y_banks, y_tiles = [], []
         for t in range(PACK):
-            m = slice(t * P, (t + 1) * P)
-            y_t = sb.tile([P, S], F32, name=f"y{t}")
-            for c in range(2):
-                bank = psum.tile([P, HALF], F32, name=f"y_ps{t}{c}", tag=f"bank{t}{c}")
-                nc.tensor.matmul_mx(
-                    out=bank[:], lhsT=ww_d[:, m].bitcast(FP8X4), lhsT_scale=ws_d[:, m],
-                    rhs=xw_g[:, cols(c)].bitcast(FP8X4), rhs_scale=xs_g[:, cols(c)], start=True, stop=True,
-                )
-                nc.scalar.copy(y_t[:, cols(c)], bank[:])
-                y_ps[t, c] = bank
-            y_sb.append(y_t)
+            y_tile = sb.tile([P, S], F32, name=f"y{t}")
+            y_bank = psum.tile([P, S], F32, name=f"y_bank{t}", tag=f"bank{t}")
+            nc.tensor.matmul_mx(
+                out=y_bank[:],
+                lhsT=w_word_dealt[:, tile_cols(t)].bitcast(FP8X4),
+                lhsT_scale=w_scale_dealt[:, tile_cols(t)],
+                rhs=picked_word[:].bitcast(FP8X4),
+                rhs_scale=picked_scale[:],
+                start=True,
+                stop=True,
+            )
+            nc.scalar.copy(y_tile[:], y_bank[:])
+            y_banks.append(y_bank)
+            y_tiles.append(y_tile)
 
         diff = sb.tile([P, PACK, S], F32)
         for t in range(PACK):
-            at_n2 = sb.tile([P, S], F32, name=f"at_n2_{t}")
-            for c in range(2):
-                nc.vector.tensor_copy(at_n2[:, cols(c)], y_sb[t][:].indirect(half(n2_l, c)))
-            for c in range(2):
+            y_at_n2 = sb.tile([P, S], F32, name=f"y_at_n2_{t}")
+            for h in range(2):
+                nc.vector.tensor_copy(y_at_n2[:, cols(h)], y_tiles[t][:].indirect(half_list(n2_list, h)))
+            for h in range(2):
                 nc.vector.tensor_tensor(
-                    diff[:, t, cols(c)], y_sb[t][:].indirect(half(n1_l, c)), at_n2[:, cols(c)], ALU.subtract
+                    diff[:, t, cols(h)],
+                    y_tiles[t][:].indirect(half_list(n1_list, h)),
+                    y_at_n2[:, cols(h)],
+                    ALU.subtract,
                 )
 
-        def scaled(out, t, factor):
-            for c in range(2):
-                nc.scalar.activation(out[:, cols(c)], y_ps[t, c][:], ACT.Copy, scale=factor[:, t : t + 1])
+        def scale_y(out, t, factor):
+            nc.scalar.activation(out, y_banks[t][:], ACT.Copy, scale=factor[:, t : t + 1])
 
-        y_gb, y_half = [], []
+        y_gb = [sb.tile([P, S], F32, name=f"y_gb{t}") for t in range(PACK)]
+        y_gb_minus_half = [sb.tile([P, S], F32, name=f"y_gb_minus_half{t}") for t in range(PACK)]
+        scale_y(y_gb[0][:], 0, gb_rows)
         for t in range(PACK):
-            y_gb_t = sb.tile([P, S], F32, name=f"y_gb{t}")
-            scaled(y_gb_t, t, gb4)
-            y_half_t = sb.tile([P, S], F32, name=f"y_half{t}")
-            scaled(y_half_t, t, gb_half)
-            y_gb.append(y_gb_t)
-            y_half.append(y_half_t)
+            if t + 1 < PACK:
+                scale_y(y_gb[t + 1][:], t + 1, gb_rows)
+            scale_y(y_gb_minus_half[t][:], t, gb_minus_half)
 
         y_ga = sb.tile([P, PACK, S], F32)
         for t in range(PACK):
-            scaled(y_ga[:, t, :], t, ga4)
-        y_ga_w = sb.tile([P, PACK, P, PACK], F32)
+            scale_y(y_ga[:, t, :], t, ga_rows)
+
+        y_ga_woven = sb.tile([P, PACK, P, PACK], F32)
         nc.scalar.copy(
-            y_ga_w[:].rearrange("p u m t -> p m t u"), y_ga[:].rearrange("p t (m u) -> p m t u", u=PACK)
+            y_ga_woven[:].rearrange("p u m t -> p m t u"), y_ga[:].rearrange("p t (m u) -> p m t u", u=PACK)
         )
-        gate_w = sb.tile([P, PACK, P, PACK], F32)
+        gate_woven = sb.tile([P, PACK, P, PACK], F32)
         nc.scalar.activation(
-            gate_w[:].rearrange("p u m t -> p m t u"), diff[:].rearrange("p t (m u) -> p m t u", u=PACK), ACT.Sigmoid
+            gate_woven[:].rearrange("p u m t -> p m t u"),
+            diff[:].rearrange("p t (m u) -> p m t u", u=PACK),
+            ACT.Sigmoid,
         )
 
-        prods = [sb.tile([P, HALF], F32, name=f"prod{i}") for i in range(3)]
-        z2_bf = []
-        for c in range(2):
-            z2_c = sb.tile([P, PACK, HALF], F32, name=f"z2_{c}")
+        products = [sb.tile([P, HALF], F32, name=f"product{i}") for i in range(PRODUCT_TILES)]
+        z2_halves, z2_woven = [], []
+        for h in range(2):
+            z2_half = sb.tile([P, PACK, HALF], F32, name=f"z2_half{h}", align_bytes=64)
             for t in range(PACK):
-                prod = prods[(c * PACK + t) % 3]
-                nc.vector.tensor_tensor(prod[:], tabs[t][:].indirect(half(n3_l, c)), y_gb[t][:, cols(c)], ALU.mult)
-                nc.vector.tensor_tensor(z2_c[:, t, :], y_half[t][:].indirect(half(n4_l, c)), prod[:], ALU.add)
-            z2_bf_c = sb.tile([P, HALF * PACK], BF16, name=f"z2_bf{c}", align_bytes=64)
+                product = products[(h * PACK + t) % PRODUCT_TILES]
+                kinds = kinds_0[:, cols(h)] if t == 0 else tab_tiles[t][:].indirect(half_list(n3_list, h))
+                nc.vector.tensor_tensor(product[:], kinds, y_gb[t][:, cols(h)], ALU.mult)
+                nc.vector.tensor_tensor(
+                    z2_half[:, t, :], y_gb_minus_half[t][:].indirect(half_list(n4_list, h)), product[:], ALU.add
+                )
+            woven = sb.tile([P, HALF * PACK], BF16, name=f"z2_woven{h}", align_bytes=64)
             nc.scalar.copy(
-                z2_bf_c[:].rearrange("p (c i t) -> p c t i", i=4, t=PACK),
-                z2_c[:].rearrange("p t (c i) -> p c t i", i=4),
+                woven[:].rearrange("p (c i t) -> p c t i", i=4, t=PACK),
+                z2_half[:].rearrange("p t (c i) -> p c t i", i=4),
             )
-            z2_bf.append(z2_bf_c)
+            z2_halves.append(z2_half)
+            z2_woven.append(woven)
 
-        z_w = sb.tile([P, S], U32, align_bytes=64)
-        z_s = sb.tile([P, S], U8, align_bytes=64)
-        z2_w = sb.tile([P, S], U32, align_bytes=64)
-        z2_s = sb.tile([P, S], U8, align_bytes=64)
-        z_bf = sb.tile([P, 2 * S], BF16, align_bytes=64)
+        z_word = sb.tile([P, S], U32, align_bytes=64)
+        z_scale = sb.tile([P, S], U8, align_bytes=64)
+        z2_word = sb.tile([P, S], U32, align_bytes=64)
+        z2_scale = sb.tile([P, S], U8, align_bytes=64)
+        z_early = sb.tile([P, 2 * S], BF16, align_bytes=64)
+        z_late = z2_halves[1][:].rearrange("p t c -> p (t c)").bitcast(BF16)
+        first, second, third, last = TILE_ORDER
+        z_rounded = {
+            first: z_early[:, 0:S],
+            second: z_early[:, S : 2 * S],
+            third: z_late[:, 0:S],
+            last: z_late[:, S : 2 * S],
+        }
 
-        def make_z(u, stage):
+        def make_z(u):
             nc.vector.tensor_tensor(
-                stage,
-                gate_w[:, u].rearrange("p m t -> p (m t)"),
-                y_ga_w[:, u].rearrange("p m t -> p (m t)"),
+                z_rounded[u],
+                gate_woven[:, u].rearrange("p m t -> p (m t)"),
+                y_ga_woven[:, u].rearrange("p m t -> p (m t)"),
                 ALU.mult,
             )
 
-        def quant_z(u, stage):
-            m = slice(u * P, (u + 1) * P)
-            nc.vector.quantize_mx(out=z_w[:, m].bitcast(FP8X4), scales=z_s[:, m], in_=stage)
-
-        def quant_z2(c):
-            nc.vector.quantize_mx(out=z2_w[:, cols(c)].bitcast(FP8X4), scales=z2_s[:, cols(c)], in_=z2_bf[c][:])
-
-        stages = [z_bf[:, 0:S], z_bf[:, S : 2 * S], z2_bf[1][:, 0:S], z2_bf[1][:, S : 2 * S]]
-        make_z(ORDER[0], stages[0])
-        quant_z2(0)
-        quant_z(ORDER[0], stages[0])
-        make_z(ORDER[1], stages[1])
-        quant_z2(1)
-        quant_z(ORDER[1], stages[1])
-        make_z(ORDER[2], stages[2])
-        make_z(ORDER[3], stages[3])
-        quant_z(ORDER[2], stages[2])
-        quant_z(ORDER[3], stages[3])
-
-        s_sb = {}
-        for u in ORDER:
-            bank = psum.tile([P, S], F32, name=f"s_ps{u}", tag=f"bank{u}0")
-            m = slice(u * P, (u + 1) * P)
-            nc.tensor.matmul_mx(
-                out=bank[:], lhsT=z_w[:, m].bitcast(FP8X4), lhsT_scale=z_s[:, m],
-                rhs=z2_w[:].bitcast(FP8X4), rhs_scale=z2_s[:], start=True, stop=True,
+        def quantize_z(u):
+            nc.vector.quantize_mx(
+                out=z_word[:, tile_cols(u)].bitcast(FP8X4), scales=z_scale[:, tile_cols(u)], in_=z_rounded[u]
             )
-            s_u = sb.tile([P, S], F32, name=f"s{u}")
-            nc.scalar.activation(s_u[:], bank[:], ACT.Copy, scale=0.0625)
-            s_sb[u] = s_u
+
+        def quantize_z2(h):
+            nc.vector.quantize_mx(
+                out=z2_word[:, cols(h)].bitcast(FP8X4), scales=z2_scale[:, cols(h)], in_=z2_woven[h][:]
+            )
+
+        for h, u in enumerate((first, second)):
+            make_z(u)
+            quantize_z2(h)
+            quantize_z(u)
+        for u in (third, last):
+            make_z(u)
+        for u in (third, last):
+            quantize_z(u)
+
+        s_tiles = {}
+        for u in TILE_ORDER:
+            s_bank = psum.tile([P, S], F32, name=f"s_bank{u}", tag=f"bank{u}")
+            nc.tensor.matmul_mx(
+                out=s_bank[:],
+                lhsT=z_word[:, tile_cols(u)].bitcast(FP8X4),
+                lhsT_scale=z_scale[:, tile_cols(u)],
+                rhs=z2_word[:].bitcast(FP8X4),
+                rhs_scale=z2_scale[:],
+                start=True,
+                stop=True,
+            )
+            s_tiles[u] = sb.tile([P, S], F32, name=f"s{u}")
+            nc.scalar.activation(s_tiles[u][:], s_bank[:], ACT.Copy, scale=0.0625)
 
         out_rows = out_0.rearrange("(p t) j -> p t j", t=PACK)
-        out_bf = sb.tile([P, S, PACK], BF16, align_bytes=64)
-        neg, gap, pos, over, res = [], [], [], [], []
+        out_woven = sb.tile([P, S, PACK], BF16, align_bytes=64)
+        minus_half_pa, lead, half_pa, relu_lead, result = [], [], [], [], []
         for u in range(PACK):
-            neg.append(sb.tile([P, HALF], F32, name=f"neg{u}"))
-            gap.append(sb.tile([P, HALF], F32, name=f"gap{u}"))
-            pos.append(sb.tile([P, HALF], F32, name=f"pos{u}"))
-            over.append(sb.tile([P, HALF], F32, name=f"over{u}"))
-            res.append(sb.tile([P, S], F32, name=f"res{u}"))
+            minus_half_pa.append(sb.tile([P, HALF], F32, name=f"minus_half_pa{u}"))
+            lead.append(sb.tile([P, HALF], F32, name=f"lead{u}"))
+            half_pa.append(sb.tile([P, HALF], F32, name=f"half_pa{u}"))
+            relu_lead.append(sb.tile([P, HALF], F32, name=f"relu_lead{u}"))
+            result.append(sb.tile([P, S], F32, name=f"result{u}"))
 
-        def fetch_a(u):
-            nc.vector.tensor_scalar(neg[u][:], s_sb[u][:].indirect(n5_l[:]), -0.5, 0.0, ALU.mult, ALU.add)
-            nc.scalar.activation(pos[u][:], neg[u][:], ACT.Copy, scale=-1.0)
+        def fetch_pa(u):
+            nc.vector.tensor_scalar(
+                minus_half_pa[u][:], s_tiles[u][:].indirect(n5_list[:]), -0.5, 0.0, ALU.mult, ALU.add
+            )
+            nc.scalar.activation(half_pa[u][:], minus_half_pa[u][:], ACT.Copy, scale=-1.0)
 
-        def fetch_b(u):
-            nc.vector.tensor_tensor(gap[u][:], s_sb[u][:].indirect(n6_l[:]), neg[u][:], ALU.add)
-            nc.scalar.activation(over[u][:], gap[u][:], ACT.Relu)
+        def fetch_pb(u):
+            nc.vector.tensor_tensor(lead[u][:], s_tiles[u][:].indirect(n6_list[:]), minus_half_pa[u][:], ALU.add)
+            nc.scalar.activation(relu_lead[u][:], lead[u][:], ACT.Relu)
 
-        def put_a(u):
-            nc.vector.tensor_tensor(res[u][:].indirect(n5_l[:]), gap[u][:], neg[u][:], ALU.add)
+        def put_ra(u):
+            nc.vector.tensor_tensor(result[u][:].indirect(n5_list[:]), lead[u][:], minus_half_pa[u][:], ALU.add)
 
-        def put_b(u):
-            nc.vector.tensor_tensor(res[u][:].indirect(n6_l[:]), over[u][:], pos[u][:], ALU.add)
-            nc.sync.dma_start(out_rows[:, u, :], res[u][:])
+        def put_rb(u):
+            nc.vector.tensor_tensor(result[u][:].indirect(n6_list[:]), relu_lead[u][:], half_pa[u][:], ALU.add)
+            nc.sync.dma_start(out_rows[:, u, :], result[u][:])
 
-        last = ORDER[-1]
-        fetch_a(ORDER[0])
-        fetch_b(ORDER[0])
-        for u, following in zip(ORDER, ORDER[1:]):
-            fetch_a(following)
-            put_a(u)
-            fetch_b(following)
+        fetch_pa(first)
+        fetch_pb(first)
+        for u, following in zip(TILE_ORDER, TILE_ORDER[1:]):
+            fetch_pa(following)
+            put_ra(u)
+            fetch_pb(following)
             if following == last:
-                put_a(last)
-            put_b(u)
-            nc.scalar.copy(out_bf[:, :, u], res[u][:])
-        put_b(last)
-        nc.vector.tensor_copy(out_bf[:, cols(0), last], res[last][:, cols(0)])
-        nc.scalar.copy(out_bf[:, cols(1), last], res[last][:, cols(1)])
+                put_ra(last)
+            put_rb(u)
+            nc.scalar.copy(out_woven[:, :, u], result[u][:])
+        put_rb(last)
+        nc.vector.tensor_copy(out_woven[:, cols(0), last], result[last][:, cols(0)])
+        nc.scalar.copy(out_woven[:, cols(1), last], result[last][:, cols(1)])
 
-        out_w = sb.tile([P, S], U32, align_bytes=64)
-        out_s = sb.tile([P, S], U8, align_bytes=64)
-        words_out = out_1[0].rearrange("p c r -> p (c r)").bitcast(I32)
-        for c in range(2):
+        out_word = sb.tile([P, S], U32, align_bytes=64)
+        out_scale = sb.tile([P, S], U8, align_bytes=64)
+        for h in range(2):
             nc.vector.quantize_mx(
-                out=out_w[:, cols(c)].bitcast(FP8X4), scales=out_s[:, cols(c)],
-                in_=out_bf[:, cols(c), :].rearrange("p c t -> p (c t)"),
+                out=out_word[:, cols(h)].bitcast(FP8X4),
+                scales=out_scale[:, cols(h)],
+                in_=out_woven[:, cols(h), :].rearrange("p c t -> p (c t)"),
             )
-            nc.sync.dma_start(words_out[:, cols(c)], out_w[:, cols(c)].bitcast(I32))
-        for q in range(4):
-            nc.scalar.dma_start(
-                out_2[0, 4 * q : 4 * q + 4, :].bitcast(I32), out_s[32 * q : 32 * q + 4, :].bitcast(I32)
-            )
+            nc.sync.dma_start(as_words(out_1)[:, cols(h)], out_word[:, cols(h)].bitcast(I32))
+        for q, queue in enumerate((nc.scalar, nc.scalar, nc.sync, nc.sync)):
+            queue.dma_start(scale_rows(out_2, q), out_scale[live_rows(q), :].bitcast(I32))

@@ -72,6 +72,9 @@ def tile_picked_selfcmpkindglift_none_po_kernel(
         load_scales(w_scale, w1_scales)
         w_word = sb.tile([P, S], I32)
         nc.sync.dma_start(w_word[:], as_words(w1_words))
+        warm = sb.tile([P, 2], F32)
+        nc.vector.memset(warm[:, 0:1], 0.0)
+        nc.scalar.activation(warm[:, 1:2], warm[:, 0:1], ACT.Sigmoid)
         tab_rows = tab.rearrange("(p t) j -> p t j", t=PACK)
         tab_tiles = [sb.tile([P, S], F32, name=f"tab{t}") for t in range(PACK)]
         n3_list = load_list(n3, "n3_list")

from contextlib import ExitStack

import concourse.mybir as mybir

F32 = mybir.dt.float32
BF16 = mybir.dt.bfloat16
I32 = mybir.dt.int32
U32 = mybir.dt.uint32
U16 = mybir.dt.uint16
U8 = mybir.dt.uint8
FP8X4 = mybir.dt.float8_e4m3fn_x4
ALU = mybir.AluOpType
ACT = mybir.ActivationFunctionType

P = 128
PACK = 4
QUADRANTS = 4
TOKENS = 2048
S = 512
HALF = S // 2
LIST_ROWS = 16
PRODUCT_TILES = 3
TILE_ORDER = (0, 2, 3, 1)
FLOPS = 2 * (2 * S * S * S)


def tile_picked_selfcmpkindglift_none_po_kernel(
    tc, x_words, x_scales, w1_words, w1_scales, tab, ga, gb, offs, n1, n2, n3, n4, n5, n6, out_0, out_1, out_2
):
    nc = tc.nc
    with ExitStack() as ctx:
        lists = ctx.enter_context(tc.tile_pool(name="lists", bufs=1))
        sb = ctx.enter_context(tc.tile_pool(name="sb", bufs=1))
        psum = ctx.enter_context(tc.psum_pool(name="psum", bufs=1))

        def load_list(source, name):
            tile = lists.tile([P, source.shape[1]], U16, name=name)
            nc.sync.dma_start(tile[:], source)
            return tile

        def live_rows(q):
            return slice(32 * q, 32 * q + 4)

        def scale_rows(scales, q):
            return scales[0, 4 * q : 4 * q + 4, :].bitcast(I32)

        def load_scales(tile, scales):
            for q in range(QUADRANTS):
                nc.sync.dma_start(tile[live_rows(q), :].bitcast(I32), scale_rows(scales, q))

        def as_words(packed):
            return packed[0].rearrange("p c r -> p (c r)").bitcast(I32)

        def cols(h):
            return slice(h * HALF, (h + 1) * HALF)

        def half_list(tile, h):
            return tile[:, h * (HALF // LIST_ROWS) : (h + 1) * (HALF // LIST_ROWS)]

        def tile_cols(t):
            return slice(t * P, (t + 1) * P)

        x_scale_window = sb.tile([P, TOKENS], U8)
        nc.vector.memset(x_scale_window[:].bitcast(I32), 0)
        w_scale = sb.tile([P, S], U8)
        nc.vector.memset(w_scale[:].bitcast(I32), 0)
        x_scale_landing = sb.tile([P, TOKENS], U8)
        load_scales(x_scale_landing, x_scales)
        offs_list = load_list(offs, "offs_list")
        x_word_window = sb.tile([P, TOKENS], U32, tag="x_words_then_kinds")
        nc.sync.dma_start(x_word_window[:].bitcast(I32), as_words(x_words))
        load_scales(w_scale, w1_scales)
        w_word = sb.tile([P, S], I32)
        nc.sync.dma_start(w_word[:], as_words(w1_words))
        warm = sb.tile([P, 2], F32)
        nc.vector.memset(warm[:, 0:1], 0.0)
        nc.scalar.activation(warm[:, 1:2], warm[:, 0:1], ACT.Sigmoid)
        tab_rows = tab.rearrange("(p t) j -> p t j", t=PACK)
        tab_tiles = [sb.tile([P, S], F32, name=f"tab{t}") for t in range(PACK)]
        n3_list = load_list(n3, "n3_list")
        nc.sync.dma_start(tab_tiles[0][:], tab_rows[:, 0, :])
        n2_list = load_list(n2, "n2_list")
        n1_list = load_list(n1, "n1_list")
        gb_rows = sb.tile([P, PACK], F32)
        nc.sync.dma_start(gb_rows[:], gb.rearrange("(p t) o -> p (t o)", t=PACK))
        ga_rows = sb.tile([P, PACK], F32)
        nc.sync.dma_start(ga_rows[:], ga.rearrange("(p t) o -> p (t o)", t=PACK))
        for t in range(1, PACK):
            nc.sync.dma_start(tab_tiles[t][:], tab_rows[:, t, :])
        n4_list = load_list(n4, "n4_list")
        n5_list = load_list(n5, "n5_list")
        n6_list = load_list(n6, "n6_list")

        for q in range(QUADRANTS):
            nc.vector.tensor_copy(
                x_scale_window[live_rows(q), :].bitcast(I32), x_scale_landing[live_rows(q), :].bitcast(I32)
            )
        picked_scale = sb.tile([P, S], U8, align_bytes=64)
        nc.vector.tensor_copy(picked_scale[:], x_scale_window[:].indirect(offs_list[:]))
        picked_word = sb.tile([P, S], U32, align_bytes=64)
        nc.vector.tensor_copy(picked_word[:], x_word_window[:].indirect(offs_list[:]))

        w_word_dealt = sb.tile([P, S], I32, align_bytes=64)
        w_scale_dealt = sb.tile([P, S], U8, align_bytes=64)
        for tiles in (slice(0, 1), slice(1, PACK)):
            for dealt, plain in ((w_scale_dealt, w_scale), (w_word_dealt, w_word)):
                nc.vector.tensor_copy(
                    dealt[:].rearrange("p (t m) -> p m t", t=PACK)[:, :, tiles],
                    plain[:].rearrange("p (m t) -> p m t", t=PACK)[:, :, tiles],
                )

        kinds_0 = sb.tile([P, S], F32, tag="x_words_then_kinds")
        for h in range(2):
            nc.vector.tensor_copy(kinds_0[:, cols(h)], tab_tiles[0][:].indirect(half_list(n3_list, h)))

        gb_minus_half = sb.tile([P, PACK], F32)
        nc.scalar.mul(gb_minus_half[:], gb_rows[:], -0.5)

        y_banks, y_tiles = [], []
        for t in range(PACK):
            y_tile = sb.tile([P, S], F32, name=f"y{t}")
            y_bank = psum.tile([P, S], F32, name=f"y_bank{t}", tag=f"bank{t}")
            nc.tensor.matmul_mx(
                out=y_bank[:],
                lhsT=w_word_dealt[:, tile_cols(t)].bitcast(FP8X4),
                lhsT_scale=w_scale_dealt[:, tile_cols(t)],
                rhs=picked_word[:].bitcast(FP8X4),
                rhs_scale=picked_scale[:],
                start=True,
                stop=True,
            )
            nc.scalar.copy(y_tile[:], y_bank[:])
            y_banks.append(y_bank)
            y_tiles.append(y_tile)

        diff = sb.tile([P, PACK, S], F32)
        for t in range(PACK):
            y_at_n2 = sb.tile([P, S], F32, name=f"y_at_n2_{t}")
            for h in range(2):
                nc.vector.tensor_copy(y_at_n2[:, cols(h)], y_tiles[t][:].indirect(half_list(n2_list, h)))
            for h in range(2):
                nc.vector.tensor_tensor(
                    diff[:, t, cols(h)],
                    y_tiles[t][:].indirect(half_list(n1_list, h)),
                    y_at_n2[:, cols(h)],
                    ALU.subtract,
                )

        def scale_y(out, t, factor):
            nc.scalar.activation(out, y_banks[t][:], ACT.Copy, scale=factor[:, t : t + 1])

        y_gb = [sb.tile([P, S], F32, name=f"y_gb{t}") for t in range(PACK)]
        y_gb_minus_half = [sb.tile([P, S], F32, name=f"y_gb_minus_half{t}") for t in range(PACK)]
        scale_y(y_gb[0][:], 0, gb_rows)
        for t in range(PACK):
            if t + 1 < PACK:
                scale_y(y_gb[t + 1][:], t + 1, gb_rows)
            scale_y(y_gb_minus_half[t][:], t, gb_minus_half)

        y_ga = sb.tile([P, PACK, S], F32)
        for t in range(PACK):
            scale_y(y_ga[:, t, :], t, ga_rows)

        y_ga_woven = sb.tile([P, PACK, P, PACK], F32)
        nc.scalar.copy(
            y_ga_woven[:].rearrange("p u m t -> p m t u"), y_ga[:].rearrange("p t (m u) -> p m t u", u=PACK)
        )
        gate_woven = sb.tile([P, PACK, P, PACK], F32)
        nc.scalar.activation(
            gate_woven[:].rearrange("p u m t -> p m t u"),
            diff[:].rearrange("p t (m u) -> p m t u", u=PACK),
            ACT.Sigmoid,
        )

        products = [sb.tile([P, HALF], F32, name=f"product{i}") for i in range(PRODUCT_TILES)]
        z2_halves, z2_woven = [], []
        for h in range(2):
            z2_half = sb.tile([P, PACK, HALF], F32, name=f"z2_half{h}", align_bytes=64)
            for t in range(PACK):
                product = products[(h * PACK + t) % PRODUCT_TILES]
                kinds = kinds_0[:, cols(h)] if t == 0 else tab_tiles[t][:].indirect(half_list(n3_list, h))
                nc.vector.tensor_tensor(product[:], kinds, y_gb[t][:, cols(h)], ALU.mult)
                nc.vector.tensor_tensor(
                    z2_half[:, t, :], y_gb_minus_half[t][:].indirect(half_list(n4_list, h)), product[:], ALU.add
                )
            woven = sb.tile([P, HALF * PACK], BF16, name=f"z2_woven{h}", align_bytes=64)
            nc.scalar.copy(
                woven[:].rearrange("p (c i t) -> p c t i", i=4, t=PACK),
                z2_half[:].rearrange("p t (c i) -> p c t i", i=4),
            )
            z2_halves.append(z2_half)
            z2_woven.append(woven)

        z_word = sb.tile([P, S], U32, align_bytes=64)
        z_scale = sb.tile([P, S], U8, align_bytes=64)
        z2_word = sb.tile([P, S], U32, align_bytes=64)
        z2_scale = sb.tile([P, S], U8, align_bytes=64)
        z_early = sb.tile([P, 2 * S], BF16, align_bytes=64)
        z_late = z2_halves[1][:].rearrange("p t c -> p (t c)").bitcast(BF16)
        first, second, third, last = TILE_ORDER
        z_rounded = {
            first: z_early[:, 0:S],
            second: z_early[:, S : 2 * S],
            third: z_late[:, 0:S],
            last: z_late[:, S : 2 * S],
        }

        def make_z(u):
            nc.vector.tensor_tensor(
                z_rounded[u],
                gate_woven[:, u].rearrange("p m t -> p (m t)"),
                y_ga_woven[:, u].rearrange("p m t -> p (m t)"),
                ALU.mult,
            )

        def quantize_z(u):
            nc.vector.quantize_mx(
                out=z_word[:, tile_cols(u)].bitcast(FP8X4), scales=z_scale[:, tile_cols(u)], in_=z_rounded[u]
            )

        def quantize_z2(h):
            nc.vector.quantize_mx(
                out=z2_word[:, cols(h)].bitcast(FP8X4), scales=z2_scale[:, cols(h)], in_=z2_woven[h][:]
            )

        for h, u in enumerate((first, second)):
            make_z(u)
            quantize_z2(h)
            quantize_z(u)
        for u in (third, last):
            make_z(u)
        for u in (third, last):
            quantize_z(u)

        s_tiles = {}
        for u in TILE_ORDER:
            s_bank = psum.tile([P, S], F32, name=f"s_bank{u}", tag=f"bank{u}")
            nc.tensor.matmul_mx(
                out=s_bank[:],
                lhsT=z_word[:, tile_cols(u)].bitcast(FP8X4),
                lhsT_scale=z_scale[:, tile_cols(u)],
                rhs=z2_word[:].bitcast(FP8X4),
                rhs_scale=z2_scale[:],
                start=True,
                stop=True,
            )
            s_tiles[u] = sb.tile([P, S], F32, name=f"s{u}")
            nc.scalar.activation(s_tiles[u][:], s_bank[:], ACT.Copy, scale=0.0625)

        out_rows = out_0.rearrange("(p t) j -> p t j", t=PACK)
        out_woven = sb.tile([P, S, PACK], BF16, align_bytes=64)
        minus_half_pa, lead, half_pa, relu_lead, result = [], [], [], [], []
        for u in range(PACK):
            minus_half_pa.append(sb.tile([P, HALF], F32, name=f"minus_half_pa{u}"))
            lead.append(sb.tile([P, HALF], F32, name=f"lead{u}"))
            half_pa.append(sb.tile([P, HALF], F32, name=f"half_pa{u}"))
            relu_lead.append(sb.tile([P, HALF], F32, name=f"relu_lead{u}"))
            result.append(sb.tile([P, S], F32, name=f"result{u}"))

        def fetch_pa(u):
            nc.vector.tensor_scalar(
                minus_half_pa[u][:], s_tiles[u][:].indirect(n5_list[:]), -0.5, 0.0, ALU.mult, ALU.add
            )
            nc.scalar.activation(half_pa[u][:], minus_half_pa[u][:], ACT.Copy, scale=-1.0)

        def fetch_pb(u):
            nc.vector.tensor_tensor(lead[u][:], s_tiles[u][:].indirect(n6_list[:]), minus_half_pa[u][:], ALU.add)
            nc.scalar.activation(relu_lead[u][:], lead[u][:], ACT.Relu)

        def put_ra(u):
            nc.vector.tensor_tensor(result[u][:].indirect(n5_list[:]), lead[u][:], minus_half_pa[u][:], ALU.add)

        def put_rb(u):
            nc.vector.tensor_tensor(result[u][:].indirect(n6_list[:]), relu_lead[u][:], half_pa[u][:], ALU.add)
            nc.sync.dma_start(out_rows[:, u, :], result[u][:])

        fetch_pa(first)
        fetch_pb(first)
        for u, following in zip(TILE_ORDER, TILE_ORDER[1:]):
            fetch_pa(following)
            put_ra(u)
            fetch_pb(following)
            if following == last:
                put_ra(last)
            put_rb(u)
            nc.scalar.copy(out_woven[:, :, u], result[u][:])
        put_rb(last)
        nc.vector.tensor_copy(out_woven[:, cols(0), last], result[last][:, cols(0)])
        nc.scalar.copy(out_woven[:, cols(1), last], result[last][:, cols(1)])

        out_word = sb.tile([P, S], U32, align_bytes=64)
        out_scale = sb.tile([P, S], U8, align_bytes=64)
        for h in range(2):
            nc.vector.quantize_mx(
                out=out_word[:, cols(h)].bitcast(FP8X4),
                scales=out_scale[:, cols(h)],
                in_=out_woven[:, cols(h), :].rearrange("p c t -> p (c t)"),
            )
            nc.sync.dma_start(as_words(out_1)[:, cols(h)], out_word[:, cols(h)].bitcast(I32))
        for q, queue in enumerate((nc.scalar, nc.scalar, nc.sync, nc.sync)):
            queue.dma_start(scale_rows(out_2, q), out_scale[live_rows(q), :].bitcast(I32))
